import numpy as np
import ml_dtypes


def mxq(x, axis, fmt="e4m3"):
    dtype, down = {"e4m3": (ml_dtypes.float8_e4m3fn, 7), "e5m2": (ml_dtypes.float8_e5m2, 14)}[fmt]
    v = np.moveaxis(np.asarray(x, np.float32).astype(ml_dtypes.bfloat16).astype(np.float64), axis, -1)
    blocks = v.reshape(v.shape[:-1] + (-1, 32))
    amax = np.abs(blocks).max(-1, keepdims=True)
    byte = np.maximum(np.where(amax > 0, np.frexp(amax)[1] - 1 + 127, 0) - down, 1)
    scale = np.exp2(byte - 127.0)
    codes = (blocks / scale).astype(np.float32).astype(dtype).astype(np.float64)
    return np.moveaxis((codes * scale).reshape(v.shape), -1, axis)


WIDE = False


def mx_kscale(k):
    if not WIDE:
        return np.ones(k)
    levels = np.array([10, -10, 5, -5, 0])
    if k % 512:
        return np.exp2(np.random.permutation(np.resize(levels, k // 32))).repeat(32)
    a = np.empty((k // 512, 16))
    for p in range(k // 512):
        a[p, :8] = np.random.permutation(np.resize(levels, 8))
        for g in range(8):
            far = levels[np.abs(levels - a[p, g]) >= 10]
            a[p, g + 8] = far[np.random.randint(len(far))]
    return np.exp2(a.ravel()).repeat(32)


def f64(x):
    return np.asarray(x).astype(np.float64)


def striped(idx):
    return np.tile(idx.reshape(-1, 16).T, (8, 1)).astype(np.uint16)


def unstriped(offs):
    return offs[:16].T.reshape(-1).astype(np.int64)


E2M1 = np.array([0.0, 0.5, 1.0, 1.5, 2.0, 3.0, 4.0, 6.0, -0.0, -0.5, -1.0, -1.5, -2.0, -3.0, -4.0, -6.0])


def pack_weight(w, fmt):
    k, n = w.shape
    w = f64(np.asarray(w, np.float32).astype(ml_dtypes.bfloat16)).reshape(k // 32, 32, n)
    amax = np.abs(w).max(1)
    if fmt == "e4m3":
        byte = np.frexp(amax)[1] - 1 + 127 - 7
    else:
        mant, ex = np.frexp(amax / 6.0)
        byte = np.where(mant > 0.5, ex, ex - 1) + 127
    byte = np.clip(np.where(amax > 0, byte, 1), 1, 254)
    scaled = (w * np.exp2(127.0 - byte)[:, None, :]).reshape(k, n).astype(np.float32)
    by_word = np.ascontiguousarray(scaled.reshape(k // 512, 128, 4, n).transpose(0, 1, 3, 2))
    if fmt == "e4m3":
        words = by_word.astype(ml_dtypes.float8_e4m3fn).view(np.uint8)
    else:
        c = by_word.astype(ml_dtypes.float4_e2m1fn).view(np.uint8) & 0xF
        words = (c[..., 0::2] | (c[..., 1::2] << 4)).reshape(k // 512, 128, 2 * n)
    return np.ascontiguousarray(words), np.ascontiguousarray(byte.astype(np.uint8).reshape(k // 512, 16, n))


def unpack_weight(words, scales, fmt):
    g, _, n = scales.shape
    words = np.ascontiguousarray(words).reshape(g, 128, n, -1)
    if fmt == "e4m3":
        vals = words.view(ml_dtypes.float8_e4m3fn).astype(np.float64)
    else:
        nib = np.empty((g, 128, n, 4), np.uint8)
        nib[..., 0::2] = words & 0xF
        nib[..., 1::2] = words >> 4
        vals = E2M1[nib]
    vals = vals * np.repeat(np.exp2(scales.astype(np.float64) - 127.0), 8, axis=1)[..., None]
    return vals.transpose(0, 1, 3, 2).reshape(g * 512, n)


def gelu(v):
    return 0.5 * v * (1.0 + np.tanh(np.sqrt(2.0 / np.pi) * (v + 0.044715 * v**3)))


K, T, S, H, M, N = 1024, 4096, 1024, 512, 512, 256


def setup_inputs():
    n = np.random.standard_normal
    s = mx_kscale(K)[:, None]
    u = mx_kscale(H)[:, None]
    u2 = mx_kscale(M)[:, None]
    d = {}
    d["tab_words"], d["tab_scales"] = pack_weight(n((K, T)) * s, "e4m3")
    d["offs"] = striped(np.random.permutation(T)[:S])
    d["xs_words"], d["xs_scales"] = pack_weight(n((K, S)) * s, "e4m3")
    d["w1"] = (n((K, H)) / K ** 0.5 / s * u.T).astype(np.float32)
    d["wx_words"], d["wx_scales"] = pack_weight(n((K, H)) / K ** 0.5 / s * u.T, "e2m1")
    d["b1"] = (0.5 * n(H) * u[:, 0]).astype(np.float32)
    d["w2"] = (1.5 * n((H, M)) / H ** 0.5 / u).astype(np.float32)
    d["b2"] = (0.7 * n(M)).astype(np.float32)
    d["gain"] = (np.exp(0.3 * n(M)) * u2[:, 0]).astype(np.float32)
    d["w3"] = (0.7 * n((K, M)) / K ** 0.5 / s * u2.T).astype(np.float32)
    d["w4_words"], d["w4_scales"] = pack_weight(n((M, N)) / M ** 0.5 / u2, "e4m3")
    return d


def reference(tab_words, tab_scales, offs, xs_words, xs_scales, w1, wx_words, wx_scales,
              b1, w2, b2, gain, w3, w4_words, w4_scales):
    v = unpack_weight(tab_words, tab_scales, "e4m3")[:, unstriped(offs)]
    xs = unpack_weight(xs_words, xs_scales, "e4m3")
    wx = unpack_weight(wx_words, wx_scales, "e2m1")
    w4 = unpack_weight(w4_words, w4_scales, "e4m3")
    both = mxq(f64(w1), 0, "e4m3").T @ v + wx.T @ xs
    h = np.maximum(both + f64(b1)[:, None], 0.0)
    e = mxq(f64(w2), 0, "e4m3").T @ mxq(h, 0, "e4m3")
    joint = np.tanh(e + f64(b2)[:, None]) * f64(gain)[:, None]
    base = mxq(f64(w3), 0, "e4m3").T @ xs
    diff = joint - base
    return w4.T @ mxq(diff, 0, "e4m3")

@@ -1,0 +1,307 @@
+from contextlib import ExitStack
+
+import concourse.mybir as mybir
+
+K, T, S, H, M, N = 1024, 4096, 1024, 512, 512, 256
+FLOPS = 2 * S * (2 * K * H + H * M + K * M + M * N)
+
+F32 = mybir.dt.float32
+BF16 = mybir.dt.bfloat16
+I32 = mybir.dt.int32
+U32 = mybir.dt.uint32
+U16 = mybir.dt.uint16
+U8 = mybir.dt.uint8
+FP8X4 = mybir.dt.float8_e4m3fn_x4
+FP4X4 = mybir.dt.float4_e2m1fn_x4
+ACT = mybir.ActivationFunctionType
+ALU = mybir.AluOpType
+
+P = 128
+PACK = 4
+KP = P * PACK
+HALF = 512
+QUARTER = 256
+TAB_ROW = (4, 8)
+
+
+def tile_list_suit_loop_contrast_kernel(
+    tc, tab_words, tab_scales, offs, xs_words, xs_scales, w1, wx_words, wx_scales,
+    b1, w2, b2, gain, w3, w4_words, w4_scales, out,
+):
+    nc = tc.nc
+    with ExitStack() as ctx:
+        keep = ctx.enter_context(tc.tile_pool(name="keep", bufs=1))
+        psum = ctx.enter_context(tc.psum_pool(name="psum", bufs=1))
+
+        slot = {"h0_woven": "w2_raw", "h1_codes": "w3_raw1"}
+
+        def sbuf(shape, dtype, name):
+            return keep.tile(shape, dtype, name=name, tag=slot.get(name, name), align_bytes=64)
+
+        def bank(b, shape, name):
+            return psum.tile(shape, F32, name=name, tag="bank%d" % b)
+
+        offsets = keep.tile([P, S // 16], U16, name="offsets")
+        nc.sync.dma_start(offsets[:], offs)
+
+        wx_plane_raw = sbuf([P, 2, H], U8, "wx_plane_raw")
+        xs_plane = sbuf([P, 2, S], U8, "xs_plane")
+        tab_plane = sbuf([P, T], U8, "tab_plane")
+        w4_plane = sbuf([P, N], U8, "w4_plane")
+        nc.gpsimd.memset(tab_plane[:].bitcast(I32), 0)
+        nc.vector.memset(wx_plane_raw[:].bitcast(I32), 0)
+        nc.vector.memset(xs_plane[:].bitcast(I32), 0)
+        nc.vector.memset(w4_plane[:].bitcast(I32), 0)
+        warm = sbuf([P, 8], F32, "warm")
+        nc.vector.memset(warm[:], 0.0)
+        warm_out = sbuf([P, 8], F32, "warm_out")
+        nc.scalar.activation(warm_out[:], warm[:], ACT.Tanh)
+
+        def load_xs(half):
+            codes = sbuf([P, 2, HALF], I32, "xs_codes%d" % half)
+            words = xs_words.rearrange("a p c i -> p a (c i)").bitcast(I32)
+            nc.sync.dma_start(codes[:], words[:, :, HALF * half : HALF * (half + 1)])
+            return codes
+
+        def load_tab(words, a, c0, c1):
+            nc.sync.dma_start(words[:, c0:c1], tab_words[a].rearrange("p t i -> p (t i)").bitcast(I32)[:, c0:c1])
+
+        def load_weight(w, a, c0, c1, name):
+            raw = sbuf([P, PACK, c1 - c0], F32, name)
+            rows = w[KP * a : KP * (a + 1), :].rearrange("(p i) c -> p i c", i=PACK)
+            nc.sync.dma_start(raw[:], rows[:, :, c0:c1])
+            return raw
+
+        def load_whole(w, a, name):
+            return load_weight(w, a, 0, KP, name)[:]
+
+        def load_halves(w, a, name):
+            return [load_weight(w, a, c, c + 256, "%s_%d" % (name, c))[:] for c in (0, 256)]
+
+        def load_channel_vector(vec, name):
+            dst = sbuf([P, PACK], F32, name)
+            nc.sync.dma_start(dst[:], vec.rearrange("(p t) -> p t", t=PACK))
+            return dst
+
+        def load_plane_rows(plane, scales, quadrants):
+            for q in quadrants:
+                nc.sync.dma_start(
+                    plane[32 * q : 32 * q + 4, :, :].bitcast(I32),
+                    scales[:, 4 * q : 4 * q + 4, :].rearrange("a r c -> r a c").bitcast(I32),
+                )
+
+        def load_tab_plane(quadrants):
+            for q in quadrants:
+                nc.sync.dma_start(
+                    tab_plane[32 * q + 4 : 32 * q + 12, :].bitcast(I32),
+                    tab_scales[:, 4 * q : 4 * q + 4, :].bitcast(I32),
+                )
+
+        tab = [sbuf([P, T], I32, "tab_codes%d" % a) for a in range(2)]
+        wx_raw = sbuf([P, 2, 2 * H], U8, "wx_raw")
+        xs_codes = [load_xs(0)]
+        nc.sync.dma_start(wx_raw[:].bitcast(I32), wx_words.rearrange("a p c -> p a c").bitcast(I32))
+        load_tab_plane((0, 1))
+        load_tab(tab[0], 0, 0, T // 2)
+        load_tab_plane((2, 3))
+        load_plane_rows(wx_plane_raw, wx_scales, (0,))
+        load_tab(tab[0], 0, T // 2, T)
+        load_plane_rows(wx_plane_raw, wx_scales, (1, 2, 3))
+        w1_raw0 = load_whole(w1, 0, "w1_raw0")
+        load_plane_rows(xs_plane, xs_scales, (0, 1, 2, 3))
+        load_tab(tab[1], 1, 0, T)
+        b1_sb = load_channel_vector(b1, "b1_sb")
+        w1_raw1 = load_halves(w1, 1, "w1_raw1")
+        w2_raw = load_whole(w2, 0, "w2_raw")
+        xs_codes.append(load_xs(1))
+        b2_sb = load_channel_vector(b2, "b2_sb")
+        gain_sb = load_channel_vector(gain, "gain_sb")
+        w3_raw0 = load_whole(w3, 0, "w3_raw0")
+        w3_raw1 = load_whole(w3, 1, "w3_raw1")
+        w4_codes = sbuf([P, N], I32, "w4_codes")
+        nc.sync.dma_start(w4_codes[:], w4_words[0].rearrange("p c i -> p (c i)").bitcast(I32))
+        for q in range(4):
+            nc.sync.dma_start(
+                w4_plane[32 * q : 32 * q + 4, :].bitcast(I32),
+                w4_scales[0, 4 * q : 4 * q + 4, :].bitcast(I32),
+            )
+
+        def copy_on(engine, dst, src):
+            if engine == "vector":
+                nc.vector.tensor_copy(dst, src)
+            elif engine == "gpsimd":
+                nc.gpsimd.tensor_scalar(dst, src, 1.0, 0.0, ALU.mult, ALU.add)
+            else:
+                nc.scalar.copy(dst, src)
+
+        def weight_tiles(name):
+            return (
+                sbuf([P, PACK, P, PACK], BF16, name + "_bf"),
+                sbuf([P, KP], I32, name + "_codes"),
+                sbuf([P, KP], U8, name + "_plane"),
+            )
+
+        def quantise_weight(name, pieces, calls):
+            grouped, codes, plane = weight_tiles(name)
+            for engine, raw, m0, t0, t1 in pieces:
+                src = raw.rearrange("p i (m t) -> p m i t", t=PACK)
+                copy_on(
+                    engine,
+                    grouped[:, t0:t1, m0 : m0 + src.shape[1], :].rearrange("p t m i -> p m i t"),
+                    src[:, :, :, t0:t1],
+                )
+            flat = grouped[:].rearrange("p t m i -> p (t m i)")
+            width = KP // calls
+            for c in range(0, KP, width):
+                nc.vector.quantize_mx(
+                    codes[:, c : c + width].bitcast(FP8X4), plane[:, c : c + width],
+                    flat[:, PACK * c : PACK * (c + width)],
+                )
+            return codes, plane
+
+        def stationary(tiles, t):
+            cols = slice(P * t, P * (t + 1))
+            return dict(lhsT=tiles[0][:, cols].bitcast(FP8X4), lhsT_scale=tiles[1][:, cols])
+
+        def xs_moving(a, half):
+            cols = slice(HALF * half, HALF * (half + 1))
+            return dict(rhs=xs_codes[half][:, a, :].bitcast(FP8X4), rhs_scale=xs_plane[:, a, cols])
+
+        wx_codes = sbuf([P, 2, 2 * H], U8, "wx_codes")
+        wx_plane = sbuf([P, 2, H], U8, "wx_plane")
+        nc.vector.tensor_copy(
+            wx_codes[:].rearrange("p a (t m b) -> p a t m b", t=PACK, b=2),
+            wx_raw[:].rearrange("p a (m t b) -> p a t m b", t=PACK, b=2),
+        )
+        nc.vector.tensor_copy(
+            wx_plane[:].rearrange("p a (t m) -> p a t m", t=PACK),
+            wx_plane_raw[:].rearrange("p a (m t) -> p a t m", t=PACK),
+        )
+
+        h_sum = [[bank(PACK * half + t, [P, HALF], "h_sum%d_%d" % (half, t)) for t in range(PACK)] for half in range(2)]
+
+        def telemetry_passes(half, t, first, last):
+            for a in range(2):
+                nc.tensor.matmul_mx(
+                    h_sum[half][t][:],
+                    lhsT=wx_codes[:, a, 2 * P * t : 2 * P * (t + 1)].bitcast(FP4X4),
+                    lhsT_scale=wx_plane[:, a, P * t : P * (t + 1)],
+                    start=(first and a == 0), stop=(last and a == 1), **xs_moving(a, half),
+                )
+
+        def table_pass(a, half, t, first, last):
+            cols = slice(HALF * half, HALF * (half + 1))
+            nc.tensor.matmul_mx(
+                h_sum[half][t][:],
+                rhs=picked[a][:, cols].bitcast(FP8X4),
+                rhs_scale=picked_plane[TAB_ROW[a] : P, cols],
+                start=first, stop=last, **stationary(w1_q[a], t),
+            )
+
+        for t in range(PACK):
+            telemetry_passes(0, t, True, False)
+
+        picked_plane = sbuf([P, S], U8, "picked_plane")
+        picked = [sbuf([P, S], I32, "picked%d" % a) for a in range(2)]
+        nc.vector.tensor_copy(picked_plane[:], tab_plane[:].indirect(offsets[:]))
+        nc.vector.tensor_copy(picked[0][:].bitcast(U32), tab[0][:].bitcast(U32).indirect(offsets[:]))
+        w1_q = [quantise_weight("w1_0", [("scalar", w1_raw0, 0, 0, PACK)], 1)]
+        for half in range(2):
+            for t in range(PACK):
+                table_pass(0, half, t, half == 1, False)
+        nc.vector.tensor_copy(picked[1][:].bitcast(U32), tab[1][:].bitcast(U32).indirect(offsets[:]))
+        w1_q.append(quantise_weight("w1_1", [("scalar", w1_raw1[0], 0, 0, PACK), ("vector", w1_raw1[1], 64, 0, PACK)], PACK))
+        for t in range(PACK):
+            table_pass(1, 0, t, False, True)
+        for t in range(PACK):
+            table_pass(1, 1, t, False, False)
+            telemetry_passes(1, t, False, True)
+
+        def weave_and_quantise(engines, planes, name):
+            width = planes.shape[2]
+            share = width // len(engines)
+            woven = sbuf([P, width, PACK], BF16, name + "_woven")
+            for s, engine in enumerate(engines):
+                cols = slice(share * s, share * (s + 1))
+                copy_on(
+                    engine,
+                    woven[:, cols, :].rearrange("p (c i) t -> p c t i", i=4),
+                    planes[:, :, cols].rearrange("p t (c i) -> p c t i", i=4),
+                )
+            codes = sbuf([P, width], I32, name + "_codes")
+            plane = sbuf([P, width], U8, name + "_plane")
+            nc.vector.quantize_mx(codes[:].bitcast(FP8X4), plane[:], woven[:].rearrange("p c t -> p (c t)"))
+            return dict(rhs=codes[:].bitcast(FP8X4), rhs_scale=plane[:])
+
+        def hidden(half, engines, on_vector=()):
+            h_bf = sbuf([P, PACK, HALF], BF16, "h_bf%d" % half)
+            for t in range(PACK):
+                if t in on_vector:
+                    nc.vector.tensor_scalar(h_bf[:, t, :], h_sum[half][t][:], b1_sb[:, t : t + 1], 0.0, ALU.add, ALU.max)
+                else:
+                    nc.scalar.activation(h_bf[:, t, :], h_sum[half][t][:], ACT.Relu, bias=b1_sb[:, t : t + 1])
+            return h_bf
+
+        bounded = [sbuf([P, PACK, HALF], F32, "bounded%d" % half) for half in range(2)]
+
+        def joint(half, moving):
+            for t in range(PACK):
+                e_sum = bank(t, [P, HALF], "e_sum%d_%d" % (half, t))
+                nc.tensor.matmul_mx(e_sum[:], start=True, stop=True, **stationary(w2_q, t), **moving)
+                nc.scalar.activation(bounded[half][:, t, :], e_sum[:], ACT.Tanh, bias=b2_sb[:, t : t + 1])
+
+        out_rows = out.rearrange("(j p) s -> p j s", p=P)
+
+        def base_sums(half):
+            sums = []
+            for t in range(PACK):
+                base = bank(PACK + t, [P, HALF], "base%d_%d" % (half, t))
+                for a in range(2):
+                    nc.tensor.matmul_mx(base[:], start=(a == 0), stop=(a == 1), **stationary(w3_q[a], t), **xs_moving(a, half))
+                sums.append(base)
+            return sums
+
+        def contrast(half, sums, c0, c1):
+            dst = sbuf([P, PACK, c1 - c0], BF16, "diff_bf%d_%d" % (half, c0))
+            for t in range(PACK):
+                nc.vector.scalar_tensor_tensor(
+                    dst[:, t, :], bounded[half][:, t, c0:c1], gain_sb[:, t : t + 1], sums[t][:, c0:c1], ALU.mult, ALU.subtract,
+                )
+            return dst
+
+        def score(moving, b, c0, c1, engine):
+            scores = bank(b, [P, 2, c1 - c0], "scores%d" % c0)
+            for j in range(2):
+                cols = slice(P * j, P * (j + 1))
+                nc.tensor.matmul_mx(
+                    scores[:, j, :], lhsT=w4_codes[:, cols].bitcast(FP8X4), lhsT_scale=w4_plane[:, cols],
+                    start=True, stop=True, **moving,
+                )
+            result = sbuf([P, 2, c1 - c0], F32, "result%d" % c0)
+            copy_on(engine, result[:], scores[:])
+            nc.sync.dma_start(out_rows[:, :, c0:c1], result[:])
+
+        h_bf0 = hidden(0, None, (1,))
+        w2_q = quantise_weight("w2", [("vector", w2_raw, 0, 0, PACK)], 1)
+        h_moving0 = weave_and_quantise(("vector",), h_bf0[:], "h0")
+        h_bf1 = hidden(1, None)
+        w3_q = [
+            quantise_weight("w3_0", [("vector", w3_raw0, 0, 0, PACK)], 1),
+            quantise_weight("w3_1", [("vector", w3_raw1, 0, 0, PACK)], 2),
+        ]
+        h_moving1 = weave_and_quantise(("scalar",), h_bf1[:], "h1")
+        joint(0, h_moving0)
+        sums0 = base_sums(0)
+        joint(1, h_moving1)
+        diff0 = contrast(0, sums0, 0, HALF)
+        sums1 = base_sums(1)
+        moving0 = weave_and_quantise(("scalar",), diff0[:, :, 0:QUARTER], "diff0")
+        diff2 = contrast(1, sums1, 0, QUARTER)
+        score(moving0, 0, 0, QUARTER, "scalar")
+        moving1 = weave_and_quantise(("scalar",), diff0[:, :, QUARTER:HALF], "diff1")
+        diff3 = contrast(1, sums1, QUARTER, HALF)
+        score(moving1, 1, QUARTER, HALF, "scalar")
+        moving2 = weave_and_quantise(("scalar",), diff2[:], "diff2")
+        moving3 = weave_and_quantise(("vector",), diff3[:], "diff3")
+        score(moving2, 2, HALF, HALF + QUARTER, "scalar")
+        score(moving3, 3, HALF + QUARTER, S, "vector")

@@ -48,7 +48,7 @@ def tile_list_suit_loop_contrast_kernel(
         xs_plane = sbuf([P, 2, S], U8, "xs_plane")
         tab_plane = sbuf([P, T], U8, "tab_plane")
         w4_plane = sbuf([P, N], U8, "w4_plane")
-        nc.gpsimd.memset(tab_plane[:].bitcast(I32), 0)
+        nc.vector.memset(tab_plane[:].bitcast(I32), 0)
         nc.vector.memset(wx_plane_raw[:].bitcast(I32), 0)
         nc.vector.memset(xs_plane[:].bitcast(I32), 0)
         nc.vector.memset(w4_plane[:].bitcast(I32), 0)
@@ -80,19 +80,19 @@ def tile_list_suit_loop_contrast_kernel(
 
         def load_channel_vector(vec, name):
             dst = sbuf([P, PACK], F32, name)
-            nc.sync.dma_start(dst[:], vec.rearrange("(p t) -> p t", t=PACK))
+            nc.gpsimd.dma_start(dst[:], vec.rearrange("(p t) -> p t", t=PACK))
             return dst
 
         def load_plane_rows(plane, scales, quadrants):
             for q in quadrants:
-                nc.sync.dma_start(
+                nc.gpsimd.dma_start(
                     plane[32 * q : 32 * q + 4, :, :].bitcast(I32),
                     scales[:, 4 * q : 4 * q + 4, :].rearrange("a r c -> r a c").bitcast(I32),
                 )
 
         def load_tab_plane(quadrants):
             for q in quadrants:
-                nc.sync.dma_start(
+                nc.gpsimd.dma_start(
                     tab_plane[32 * q + 4 : 32 * q + 12, :].bitcast(I32),
                     tab_scales[:, 4 * q : 4 * q + 4, :].bitcast(I32),
                 )
@@ -101,27 +101,24 @@ def tile_list_suit_loop_contrast_kernel(
         wx_raw = sbuf([P, 2, 2 * H], U8, "wx_raw")
         xs_codes = [load_xs(0)]
         nc.sync.dma_start(wx_raw[:].bitcast(I32), wx_words.rearrange("a p c -> p a c").bitcast(I32))
-        load_tab_plane((0, 1))
-        load_tab(tab[0], 0, 0, T // 2)
-        load_tab_plane((2, 3))
-        load_plane_rows(wx_plane_raw, wx_scales, (0,))
-        load_tab(tab[0], 0, T // 2, T)
-        load_plane_rows(wx_plane_raw, wx_scales, (1, 2, 3))
-        w1_raw0 = load_whole(w1, 0, "w1_raw0")
+        load_tab_plane((0, 1, 2, 3))
+        load_plane_rows(wx_plane_raw, wx_scales, (0, 1, 2, 3))
         load_plane_rows(xs_plane, xs_scales, (0, 1, 2, 3))
-        load_tab(tab[1], 1, 0, T)
         b1_sb = load_channel_vector(b1, "b1_sb")
-        w1_raw1 = load_halves(w1, 1, "w1_raw1")
-        w2_raw = load_whole(w2, 0, "w2_raw")
-        xs_codes.append(load_xs(1))
         b2_sb = load_channel_vector(b2, "b2_sb")
         gain_sb = load_channel_vector(gain, "gain_sb")
+        load_tab(tab[0], 0, 0, T)
+        w1_raw0 = load_whole(w1, 0, "w1_raw0")
+        load_tab(tab[1], 1, 0, T)
+        w1_raw1 = load_whole(w1, 1, "w1_raw1")
+        w2_raw = load_whole(w2, 0, "w2_raw")
+        xs_codes.append(load_xs(1))
         w3_raw0 = load_whole(w3, 0, "w3_raw0")
         w3_raw1 = load_whole(w3, 1, "w3_raw1")
         w4_codes = sbuf([P, N], I32, "w4_codes")
         nc.sync.dma_start(w4_codes[:], w4_words[0].rearrange("p c i -> p (c i)").bitcast(I32))
         for q in range(4):
-            nc.sync.dma_start(
+            nc.gpsimd.dma_start(
                 w4_plane[32 * q : 32 * q + 4, :].bitcast(I32),
                 w4_scales[0, 4 * q : 4 * q + 4, :].bitcast(I32),
             )
@@ -210,7 +207,7 @@ def tile_list_suit_loop_contrast_kernel(
             for t in range(PACK):
                 table_pass(0, half, t, half == 1, False)
         nc.vector.tensor_copy(picked[1][:].bitcast(U32), tab[1][:].bitcast(U32).indirect(offsets[:]))
-        w1_q.append(quantise_weight("w1_1", [("scalar", w1_raw1[0], 0, 0, PACK), ("vector", w1_raw1[1], 64, 0, PACK)], PACK))
+        w1_q.append(quantise_weight("w1_1", [("vector", w1_raw1, 0, 0, 2), ("scalar", w1_raw1, 0, 2, PACK)], 2))
         for t in range(PACK):
             table_pass(1, 0, t, False, True)
         for t in range(PACK):

@@ -49,8 +49,8 @@ def tile_list_suit_loop_contrast_kernel(
         tab_plane = sbuf([P, T], U8, "tab_plane")
         w4_plane = sbuf([P, N], U8, "w4_plane")
         nc.vector.memset(tab_plane[:].bitcast(I32), 0)
-        nc.vector.memset(wx_plane_raw[:].bitcast(I32), 0)
-        nc.vector.memset(xs_plane[:].bitcast(I32), 0)
+        nc.gpsimd.memset(wx_plane_raw[:].bitcast(I32), 0)
+        nc.gpsimd.memset(xs_plane[:].bitcast(I32), 0)
         nc.vector.memset(w4_plane[:].bitcast(I32), 0)
         warm = sbuf([P, 8], F32, "warm")
         nc.vector.memset(warm[:], 0.0)
@@ -80,48 +80,47 @@ def tile_list_suit_loop_contrast_kernel(
 
         def load_channel_vector(vec, name):
             dst = sbuf([P, PACK], F32, name)
-            nc.gpsimd.dma_start(dst[:], vec.rearrange("(p t) -> p t", t=PACK))
+            nc.sync.dma_start(dst[:], vec.rearrange("(p t) -> p t", t=PACK))
             return dst
 
-        def load_plane_rows(plane, scales, quadrants):
-            for q in quadrants:
-                nc.gpsimd.dma_start(
-                    plane[32 * q : 32 * q + 4, :, :].bitcast(I32),
-                    scales[:, 4 * q : 4 * q + 4, :].rearrange("a r c -> r a c").bitcast(I32),
+        def load_plane_rows(plane, scales):
+            for r in range(4):
+                nc.sync.dma_start(
+                    plane[r:P:32, :, :].bitcast(I32),
+                    scales[:, r:16:4, :].rearrange("a q c -> q a c").bitcast(I32),
                 )
 
-        def load_tab_plane(quadrants):
-            for q in quadrants:
-                nc.gpsimd.dma_start(
-                    tab_plane[32 * q + 4 : 32 * q + 12, :].bitcast(I32),
-                    tab_scales[:, 4 * q : 4 * q + 4, :].bitcast(I32),
+        def load_tab_plane(a):
+            for r in range(4):
+                nc.sync.dma_start(
+                    tab_plane[TAB_ROW[a] + r : P : 32, :].bitcast(I32),
+                    tab_scales[a, r:16:4, :].bitcast(I32),
                 )
 
         tab = [sbuf([P, T], I32, "tab_codes%d" % a) for a in range(2)]
         wx_raw = sbuf([P, 2, 2 * H], U8, "wx_raw")
         xs_codes = [load_xs(0)]
         nc.sync.dma_start(wx_raw[:].bitcast(I32), wx_words.rearrange("a p c -> p a c").bitcast(I32))
-        load_tab_plane((0, 1, 2, 3))
-        load_plane_rows(wx_plane_raw, wx_scales, (0, 1, 2, 3))
-        load_plane_rows(xs_plane, xs_scales, (0, 1, 2, 3))
-        b1_sb = load_channel_vector(b1, "b1_sb")
-        b2_sb = load_channel_vector(b2, "b2_sb")
-        gain_sb = load_channel_vector(gain, "gain_sb")
-        load_tab(tab[0], 0, 0, T)
+        load_tab_plane(0)
+        load_tab(tab[0], 0, 0, T // 2)
+        load_tab_plane(1)
+        load_tab(tab[0], 0, T // 2, T)
+        load_plane_rows(wx_plane_raw, wx_scales)
         w1_raw0 = load_whole(w1, 0, "w1_raw0")
+        load_plane_rows(xs_plane, xs_scales)
         load_tab(tab[1], 1, 0, T)
+        b1_sb = load_channel_vector(b1, "b1_sb")
         w1_raw1 = load_whole(w1, 1, "w1_raw1")
         w2_raw = load_whole(w2, 0, "w2_raw")
         xs_codes.append(load_xs(1))
+        b2_sb = load_channel_vector(b2, "b2_sb")
+        gain_sb = load_channel_vector(gain, "gain_sb")
         w3_raw0 = load_whole(w3, 0, "w3_raw0")
         w3_raw1 = load_whole(w3, 1, "w3_raw1")
         w4_codes = sbuf([P, N], I32, "w4_codes")
         nc.sync.dma_start(w4_codes[:], w4_words[0].rearrange("p c i -> p (c i)").bitcast(I32))
-        for q in range(4):
-            nc.gpsimd.dma_start(
-                w4_plane[32 * q : 32 * q + 4, :].bitcast(I32),
-                w4_scales[0, 4 * q : 4 * q + 4, :].bitcast(I32),
-            )
+        for r in range(4):
+            nc.sync.dma_start(w4_plane[r:P:32, :].bitcast(I32), w4_scales[0, r:16:4, :].bitcast(I32))
 
         def copy_on(engine, dst, src):
             if engine == "vector":

@@ -46,9 +46,12 @@ def tile_list_suit_loop_contrast_kernel(
 
         wx_plane_raw = sbuf([P, 2, H], U8, "wx_plane_raw")
         xs_plane = sbuf([P, 2, S], U8, "xs_plane")
-        tab_plane = sbuf([P, T], U8, "tab_plane")
+        tab_rows = sbuf([P, T], U8, "tab_rows")
+        picked_plane = [sbuf([P, S], U8, "picked_plane%d" % a) for a in range(2)]
         w4_plane = sbuf([P, N], U8, "w4_plane")
-        nc.vector.memset(tab_plane[:].bitcast(I32), 0)
+        nc.vector.memset(tab_rows[:].bitcast(I32), 0)
+        nc.vector.memset(picked_plane[0][:].bitcast(I32), 0)
+        nc.vector.memset(picked_plane[1][:].bitcast(I32), 0)
         nc.gpsimd.memset(wx_plane_raw[:].bitcast(I32), 0)
         nc.gpsimd.memset(xs_plane[:].bitcast(I32), 0)
         nc.vector.memset(w4_plane[:].bitcast(I32), 0)
@@ -90,27 +93,32 @@ def tile_list_suit_loop_contrast_kernel(
                     scales[:, r:16:4, :].rearrange("a q c -> q a c").bitcast(I32),
                 )
 
-        def load_tab_plane(a):
-            for r in range(4):
+        def place_picked_rows(a, rows):
+            for r in rows:
+                first = 4 * (16 * a + r)
                 nc.sync.dma_start(
-                    tab_plane[TAB_ROW[a] + r : P : 32, :].bitcast(I32),
-                    tab_scales[a, r:16:4, :].bitcast(I32),
+                    picked_plane[a][TAB_ROW[a] + r : P : 32, :].bitcast(I32),
+                    picked_rows[first : first + 49 : 16, :].bitcast(I32),
                 )
 
         tab = [sbuf([P, T], I32, "tab_codes%d" % a) for a in range(2)]
         wx_raw = sbuf([P, 2, 2 * H], U8, "wx_raw")
+        nc.sync.dma_start(tab_rows[0:P:4, :].bitcast(I32), tab_scales.rearrange("a q c -> (a q) c").bitcast(I32))
+        picked_rows = sbuf([P, S], U8, "picked_rows")
+        nc.vector.tensor_copy(picked_rows[:], tab_rows[:].indirect(offsets[:]))
         xs_codes = [load_xs(0)]
         nc.sync.dma_start(wx_raw[:].bitcast(I32), wx_words.rearrange("a p c -> p a c").bitcast(I32))
-        load_tab_plane(0)
         load_tab(tab[0], 0, 0, T // 2)
-        load_tab_plane(1)
-        load_tab(tab[0], 0, T // 2, T)
         load_plane_rows(wx_plane_raw, wx_scales)
+        load_tab(tab[0], 0, T // 2, T)
         w1_raw0 = load_whole(w1, 0, "w1_raw0")
+        place_picked_rows(0, range(4))
+        load_tab(tab[1], 1, 0, T // 2)
+        place_picked_rows(1, range(4))
+        load_tab(tab[1], 1, T // 2, T)
         load_plane_rows(xs_plane, xs_scales)
-        load_tab(tab[1], 1, 0, T)
-        b1_sb = load_channel_vector(b1, "b1_sb")
         w1_raw1 = load_whole(w1, 1, "w1_raw1")
+        b1_sb = load_channel_vector(b1, "b1_sb")
         w2_raw = load_whole(w2, 0, "w2_raw")
         xs_codes.append(load_xs(1))
         b2_sb = load_channel_vector(b2, "b2_sb")
@@ -190,21 +198,18 @@ def tile_list_suit_loop_contrast_kernel(
             nc.tensor.matmul_mx(
                 h_sum[half][t][:],
                 rhs=picked[a][:, cols].bitcast(FP8X4),
-                rhs_scale=picked_plane[TAB_ROW[a] : P, cols],
+                rhs_scale=picked_plane[a][TAB_ROW[a] : P, cols],
                 start=first, stop=last, **stationary(w1_q[a], t),
             )
 
-        for t in range(PACK):
-            telemetry_passes(0, t, True, False)
-
-        picked_plane = sbuf([P, S], U8, "picked_plane")
         picked = [sbuf([P, S], I32, "picked%d" % a) for a in range(2)]
-        nc.vector.tensor_copy(picked_plane[:], tab_plane[:].indirect(offsets[:]))
         nc.vector.tensor_copy(picked[0][:].bitcast(U32), tab[0][:].bitcast(U32).indirect(offsets[:]))
         w1_q = [quantise_weight("w1_0", [("scalar", w1_raw0, 0, 0, PACK)], 1)]
         for half in range(2):
             for t in range(PACK):
-                table_pass(0, half, t, half == 1, False)
+                table_pass(0, half, t, True, False)
+        for t in range(PACK):
+            telemetry_passes(0, t, False, False)
         nc.vector.tensor_copy(picked[1][:].bitcast(U32), tab[1][:].bitcast(U32).indirect(offsets[:]))
         w1_q.append(quantise_weight("w1_1", [("vector", w1_raw1, 0, 0, 2), ("scalar", w1_raw1, 0, 2, PACK)], 2))
         for t in range(PACK):
@@ -291,7 +296,7 @@ def tile_list_suit_loop_contrast_kernel(
         joint(1, h_moving1)
         diff0 = contrast(0, sums0, 0, HALF)
         sums1 = base_sums(1)
-        moving0 = weave_and_quantise(("scalar",), diff0[:, :, 0:QUARTER], "diff0")
+        moving0 = weave_and_quantise(("vector",), diff0[:, :, 0:QUARTER], "diff0")
         diff2 = contrast(1, sums1, 0, QUARTER)
         score(moving0, 0, 0, QUARTER, "scalar")
         moving1 = weave_and_quantise(("scalar",), diff0[:, :, QUARTER:HALF], "diff1")

@@ -19,9 +19,15 @@ ALU = mybir.AluOpType
 P = 128
 PACK = 4
 KP = P * PACK
-HALF = 512
-QUARTER = 256
-TAB_ROW = (4, 8)
+QUADRANT = 32
+PLANE_ROWS = 4
+BLOCKS = 16
+PASSES = K // KP
+HALF = S // 2
+QUARTER = S // 4
+RUN = 4
+ROW_STEP = 4
+PICKED_START = (4, 8)
 
 
 def tile_list_suit_loop_contrast_kernel(
@@ -33,10 +39,10 @@ def tile_list_suit_loop_contrast_kernel(
         keep = ctx.enter_context(tc.tile_pool(name="keep", bufs=1))
         psum = ctx.enter_context(tc.psum_pool(name="psum", bufs=1))
 
-        slot = {"h0_woven": "w2_raw", "h1_codes": "w3_raw1"}
+        reuses = {"h0_woven": "w2_raw", "h1_codes": "w3_raw1"}
 
         def sbuf(shape, dtype, name):
-            return keep.tile(shape, dtype, name=name, tag=slot.get(name, name), align_bytes=64)
+            return keep.tile(shape, dtype, name=name, tag=reuses.get(name, name), align_bytes=64)
 
         def bank(b, shape, name):
             return psum.tile(shape, F32, name=name, tag="bank%d" % b)
@@ -44,42 +50,33 @@ def tile_list_suit_loop_contrast_kernel(
         offsets = keep.tile([P, S // 16], U16, name="offsets")
         nc.sync.dma_start(offsets[:], offs)
 
-        wx_plane_raw = sbuf([P, 2, H], U8, "wx_plane_raw")
-        xs_plane = sbuf([P, 2, S], U8, "xs_plane")
+        wx_plane_raw = sbuf([P, PASSES, H], U8, "wx_plane_raw")
+        xs_plane = sbuf([P, PASSES, S], U8, "xs_plane")
         tab_rows = sbuf([P, T], U8, "tab_rows")
-        picked_plane = [sbuf([P, S], U8, "picked_plane%d" % a) for a in range(2)]
+        picked_plane = [sbuf([P, S], U8, "picked_plane%d" % a) for a in range(PASSES)]
         w4_plane = sbuf([P, N], U8, "w4_plane")
         nc.vector.memset(tab_rows[:].bitcast(I32), 0)
-        nc.vector.memset(picked_plane[0][:].bitcast(I32), 0)
-        nc.vector.memset(picked_plane[1][:].bitcast(I32), 0)
+        for a in range(PASSES):
+            nc.vector.memset(picked_plane[a][:].bitcast(I32), 0)
         nc.gpsimd.memset(wx_plane_raw[:].bitcast(I32), 0)
         nc.gpsimd.memset(xs_plane[:].bitcast(I32), 0)
         nc.vector.memset(w4_plane[:].bitcast(I32), 0)
-        warm = sbuf([P, 8], F32, "warm")
-        nc.vector.memset(warm[:], 0.0)
-        warm_out = sbuf([P, 8], F32, "warm_out")
-        nc.scalar.activation(warm_out[:], warm[:], ACT.Tanh)
 
         def load_xs(half):
-            codes = sbuf([P, 2, HALF], I32, "xs_codes%d" % half)
+            codes = sbuf([P, PASSES, HALF], I32, "xs_codes%d" % half)
             words = xs_words.rearrange("a p c i -> p a (c i)").bitcast(I32)
             nc.sync.dma_start(codes[:], words[:, :, HALF * half : HALF * (half + 1)])
             return codes
 
-        def load_tab(words, a, c0, c1):
-            nc.sync.dma_start(words[:, c0:c1], tab_words[a].rearrange("p t i -> p (t i)").bitcast(I32)[:, c0:c1])
+        def load_table(a):
+            words = sbuf([P, T], I32, "tab_codes%d" % a)
+            nc.sync.dma_start(words[:], tab_words[a].rearrange("p t i -> p (t i)").bitcast(I32))
+            return words
 
-        def load_weight(w, a, c0, c1, name):
-            raw = sbuf([P, PACK, c1 - c0], F32, name)
-            rows = w[KP * a : KP * (a + 1), :].rearrange("(p i) c -> p i c", i=PACK)
-            nc.sync.dma_start(raw[:], rows[:, :, c0:c1])
+        def load_weight(w, a, name):
+            raw = sbuf([P, PACK, KP], F32, name)
+            nc.sync.dma_start(raw[:], w[KP * a : KP * (a + 1), :].rearrange("(p i) c -> p i c", i=PACK))
             return raw
-
-        def load_whole(w, a, name):
-            return load_weight(w, a, 0, KP, name)[:]
-
-        def load_halves(w, a, name):
-            return [load_weight(w, a, c, c + 256, "%s_%d" % (name, c))[:] for c in (0, 256)]
 
         def load_channel_vector(vec, name):
             dst = sbuf([P, PACK], F32, name)
@@ -87,157 +84,139 @@ def tile_list_suit_loop_contrast_kernel(
             return dst
 
         def load_plane_rows(plane, scales):
-            for r in range(4):
+            for r in range(PLANE_ROWS):
                 nc.sync.dma_start(
-                    plane[r:P:32, :, :].bitcast(I32),
-                    scales[:, r:16:4, :].rearrange("a q c -> q a c").bitcast(I32),
+                    plane[r:P:QUADRANT, :, :].bitcast(I32),
+                    scales[:, r:BLOCKS:PLANE_ROWS, :].rearrange("a q c -> q a c").bitcast(I32),
                 )
 
-        def place_picked_rows(a, rows):
-            for r in rows:
-                first = 4 * (16 * a + r)
+        def place_picked_rows(a):
+            step = ROW_STEP * PLANE_ROWS
+            for r in range(PLANE_ROWS):
+                first = ROW_STEP * (BLOCKS * a + r)
                 nc.sync.dma_start(
-                    picked_plane[a][TAB_ROW[a] + r : P : 32, :].bitcast(I32),
-                    picked_rows[first : first + 49 : 16, :].bitcast(I32),
+                    picked_plane[a][PICKED_START[a] + r : P : QUADRANT, :].bitcast(I32),
+                    picked_rows[first : first + 3 * step + 1 : step, :].bitcast(I32),
                 )
 
-        tab = [sbuf([P, T], I32, "tab_codes%d" % a) for a in range(2)]
-        wx_raw = sbuf([P, 2, 2 * H], U8, "wx_raw")
-        nc.sync.dma_start(tab_rows[0:P:4, :].bitcast(I32), tab_scales.rearrange("a q c -> (a q) c").bitcast(I32))
+        nc.sync.dma_start(tab_rows[0:P:ROW_STEP, :].bitcast(I32), tab_scales.rearrange("a q c -> (a q) c").bitcast(I32))
         picked_rows = sbuf([P, S], U8, "picked_rows")
         nc.vector.tensor_copy(picked_rows[:], tab_rows[:].indirect(offsets[:]))
         xs_codes = [load_xs(0)]
+        wx_raw = sbuf([P, PASSES, 2 * H], U8, "wx_raw")
         nc.sync.dma_start(wx_raw[:].bitcast(I32), wx_words.rearrange("a p c -> p a c").bitcast(I32))
-        load_tab(tab[0], 0, 0, T // 2)
+        w1_raw = [load_weight(w1, 0, "w1_raw0")]
         load_plane_rows(wx_plane_raw, wx_scales)
-        load_tab(tab[0], 0, T // 2, T)
-        w1_raw0 = load_whole(w1, 0, "w1_raw0")
-        place_picked_rows(0, range(4))
-        load_tab(tab[1], 1, 0, T // 2)
-        place_picked_rows(1, range(4))
-        load_tab(tab[1], 1, T // 2, T)
+        tab = [load_table(0)]
+        place_picked_rows(0)
+        tab.append(load_table(1))
         load_plane_rows(xs_plane, xs_scales)
-        w1_raw1 = load_whole(w1, 1, "w1_raw1")
+        w1_raw.append(load_weight(w1, 1, "w1_raw1"))
+        place_picked_rows(1)
+        w2_raw = load_weight(w2, 0, "w2_raw")
         b1_sb = load_channel_vector(b1, "b1_sb")
-        w2_raw = load_whole(w2, 0, "w2_raw")
         xs_codes.append(load_xs(1))
         b2_sb = load_channel_vector(b2, "b2_sb")
         gain_sb = load_channel_vector(gain, "gain_sb")
-        w3_raw0 = load_whole(w3, 0, "w3_raw0")
-        w3_raw1 = load_whole(w3, 1, "w3_raw1")
+        w3_raw = [load_weight(w3, a, "w3_raw%d" % a) for a in range(PASSES)]
         w4_codes = sbuf([P, N], I32, "w4_codes")
         nc.sync.dma_start(w4_codes[:], w4_words[0].rearrange("p c i -> p (c i)").bitcast(I32))
-        for r in range(4):
-            nc.sync.dma_start(w4_plane[r:P:32, :].bitcast(I32), w4_scales[0, r:16:4, :].bitcast(I32))
+        for r in range(PLANE_ROWS):
+            nc.sync.dma_start(w4_plane[r:P:QUADRANT, :].bitcast(I32), w4_scales[0, r:BLOCKS:PLANE_ROWS, :].bitcast(I32))
 
-        def copy_on(engine, dst, src):
-            if engine == "vector":
-                nc.vector.tensor_copy(dst, src)
-            elif engine == "gpsimd":
-                nc.gpsimd.tensor_scalar(dst, src, 1.0, 0.0, ALU.mult, ALU.add)
-            else:
-                nc.scalar.copy(dst, src)
+        on_vector = nc.vector.tensor_copy
+        on_scalar = nc.scalar.copy
 
-        def weight_tiles(name):
-            return (
-                sbuf([P, PACK, P, PACK], BF16, name + "_bf"),
-                sbuf([P, KP], I32, name + "_codes"),
-                sbuf([P, KP], U8, name + "_plane"),
-            )
-
-        def quantise_weight(name, pieces, calls):
-            grouped, codes, plane = weight_tiles(name)
-            for engine, raw, m0, t0, t1 in pieces:
-                src = raw.rearrange("p i (m t) -> p m i t", t=PACK)
-                copy_on(
-                    engine,
-                    grouped[:, t0:t1, m0 : m0 + src.shape[1], :].rearrange("p t m i -> p m i t"),
-                    src[:, :, :, t0:t1],
-                )
-            flat = grouped[:].rearrange("p t m i -> p (t m i)")
+        def quantise_weight(name, raw, copies, calls):
+            grouped = sbuf([P, PACK, P, PACK], BF16, name + "_bf")
+            codes = sbuf([P, KP], I32, name + "_codes")
+            plane = sbuf([P, KP], U8, name + "_plane")
+            src = raw[:].rearrange("p i (c t) -> p c i t", t=PACK)
+            share = PACK // len(copies)
+            for s, copy in enumerate(copies):
+                tiles = slice(share * s, share * (s + 1))
+                copy(grouped[:, tiles, :, :].rearrange("p t c i -> p c i t"), src[:, :, :, tiles])
+            flat = grouped[:].rearrange("p t c i -> p (t c i)")
             width = KP // calls
-            for c in range(0, KP, width):
+            for first in range(0, KP, width):
                 nc.vector.quantize_mx(
-                    codes[:, c : c + width].bitcast(FP8X4), plane[:, c : c + width],
-                    flat[:, PACK * c : PACK * (c + width)],
+                    codes[:, first : first + width].bitcast(FP8X4), plane[:, first : first + width],
+                    flat[:, PACK * first : PACK * (first + width)],
                 )
             return codes, plane
 
-        def stationary(tiles, t):
+        def stationary(quantised, t):
+            codes, plane = quantised
             cols = slice(P * t, P * (t + 1))
-            return dict(lhsT=tiles[0][:, cols].bitcast(FP8X4), lhsT_scale=tiles[1][:, cols])
+            return dict(lhsT=codes[:, cols].bitcast(FP8X4), lhsT_scale=plane[:, cols])
 
         def xs_moving(a, half):
             cols = slice(HALF * half, HALF * (half + 1))
             return dict(rhs=xs_codes[half][:, a, :].bitcast(FP8X4), rhs_scale=xs_plane[:, a, cols])
 
-        wx_codes = sbuf([P, 2, 2 * H], U8, "wx_codes")
-        wx_plane = sbuf([P, 2, H], U8, "wx_plane")
+        wx_codes = sbuf([P, PASSES, 2 * H], U8, "wx_codes")
+        wx_plane = sbuf([P, PASSES, H], U8, "wx_plane")
         nc.vector.tensor_copy(
-            wx_codes[:].rearrange("p a (t m b) -> p a t m b", t=PACK, b=2),
-            wx_raw[:].rearrange("p a (m t b) -> p a t m b", t=PACK, b=2),
+            wx_codes[:].rearrange("p a (t c b) -> p a t c b", t=PACK, b=2),
+            wx_raw[:].rearrange("p a (c t b) -> p a t c b", t=PACK, b=2),
         )
         nc.vector.tensor_copy(
-            wx_plane[:].rearrange("p a (t m) -> p a t m", t=PACK),
-            wx_plane_raw[:].rearrange("p a (m t) -> p a t m", t=PACK),
+            wx_plane[:].rearrange("p a (t c) -> p a t c", t=PACK),
+            wx_plane_raw[:].rearrange("p a (c t) -> p a t c", t=PACK),
         )
 
         h_sum = [[bank(PACK * half + t, [P, HALF], "h_sum%d_%d" % (half, t)) for t in range(PACK)] for half in range(2)]
 
-        def telemetry_passes(half, t, first, last):
-            for a in range(2):
+        def telemetry_passes(half, t, closes):
+            for a in range(PASSES):
                 nc.tensor.matmul_mx(
                     h_sum[half][t][:],
                     lhsT=wx_codes[:, a, 2 * P * t : 2 * P * (t + 1)].bitcast(FP4X4),
                     lhsT_scale=wx_plane[:, a, P * t : P * (t + 1)],
-                    start=(first and a == 0), stop=(last and a == 1), **xs_moving(a, half),
+                    start=False, stop=(closes and a == PASSES - 1), **xs_moving(a, half),
                 )
 
-        def table_pass(a, half, t, first, last):
+        def table_pass(a, half, t, closes):
             cols = slice(HALF * half, HALF * (half + 1))
             nc.tensor.matmul_mx(
                 h_sum[half][t][:],
                 rhs=picked[a][:, cols].bitcast(FP8X4),
-                rhs_scale=picked_plane[a][TAB_ROW[a] : P, cols],
-                start=first, stop=last, **stationary(w1_q[a], t),
+                rhs_scale=picked_plane[a][PICKED_START[a] : P, cols],
+                start=(a == 0), stop=closes, **stationary(w1_q[a], t),
             )
 
-        picked = [sbuf([P, S], I32, "picked%d" % a) for a in range(2)]
+        picked = [sbuf([P, S], I32, "picked%d" % a) for a in range(PASSES)]
         nc.vector.tensor_copy(picked[0][:].bitcast(U32), tab[0][:].bitcast(U32).indirect(offsets[:]))
-        w1_q = [quantise_weight("w1_0", [("scalar", w1_raw0, 0, 0, PACK)], 1)]
+        w1_q = [quantise_weight("w1_0", w1_raw[0], (on_scalar,), 1)]
         for half in range(2):
             for t in range(PACK):
-                table_pass(0, half, t, True, False)
+                table_pass(0, half, t, False)
         for t in range(PACK):
-            telemetry_passes(0, t, False, False)
+            telemetry_passes(0, t, False)
         nc.vector.tensor_copy(picked[1][:].bitcast(U32), tab[1][:].bitcast(U32).indirect(offsets[:]))
-        w1_q.append(quantise_weight("w1_1", [("vector", w1_raw1, 0, 0, 2), ("scalar", w1_raw1, 0, 2, PACK)], 2))
+        w1_q.append(quantise_weight("w1_1", w1_raw[1], (on_vector, on_scalar), 2))
         for t in range(PACK):
-            table_pass(1, 0, t, False, True)
+            table_pass(1, 0, t, True)
         for t in range(PACK):
-            table_pass(1, 1, t, False, False)
-            telemetry_passes(1, t, False, True)
+            table_pass(1, 1, t, False)
+            telemetry_passes(1, t, True)
 
-        def weave_and_quantise(engines, planes, name):
-            width = planes.shape[2]
-            share = width // len(engines)
+        def weave_and_quantise(copy, tiles, name):
+            width = tiles.shape[2]
             woven = sbuf([P, width, PACK], BF16, name + "_woven")
-            for s, engine in enumerate(engines):
-                cols = slice(share * s, share * (s + 1))
-                copy_on(
-                    engine,
-                    woven[:, cols, :].rearrange("p (c i) t -> p c t i", i=4),
-                    planes[:, :, cols].rearrange("p t (c i) -> p c t i", i=4),
-                )
+            copy(
+                woven[:].rearrange("p (c i) t -> p c t i", i=RUN),
+                tiles.rearrange("p t (c i) -> p c t i", i=RUN),
+            )
             codes = sbuf([P, width], I32, name + "_codes")
             plane = sbuf([P, width], U8, name + "_plane")
             nc.vector.quantize_mx(codes[:].bitcast(FP8X4), plane[:], woven[:].rearrange("p c t -> p (c t)"))
             return dict(rhs=codes[:].bitcast(FP8X4), rhs_scale=plane[:])
 
-        def hidden(half, engines, on_vector=()):
+        def hidden(half, vector_tiles):
             h_bf = sbuf([P, PACK, HALF], BF16, "h_bf%d" % half)
             for t in range(PACK):
-                if t in on_vector:
+                if t in vector_tiles:
                     nc.vector.tensor_scalar(h_bf[:, t, :], h_sum[half][t][:], b1_sb[:, t : t + 1], 0.0, ALU.add, ALU.max)
                 else:
                     nc.scalar.activation(h_bf[:, t, :], h_sum[half][t][:], ACT.Relu, bias=b1_sb[:, t : t + 1])
@@ -251,14 +230,14 @@ def tile_list_suit_loop_contrast_kernel(
                 nc.tensor.matmul_mx(e_sum[:], start=True, stop=True, **stationary(w2_q, t), **moving)
                 nc.scalar.activation(bounded[half][:, t, :], e_sum[:], ACT.Tanh, bias=b2_sb[:, t : t + 1])
 
-        out_rows = out.rearrange("(j p) s -> p j s", p=P)
-
         def base_sums(half):
             sums = []
             for t in range(PACK):
                 base = bank(PACK + t, [P, HALF], "base%d_%d" % (half, t))
-                for a in range(2):
-                    nc.tensor.matmul_mx(base[:], start=(a == 0), stop=(a == 1), **stationary(w3_q[a], t), **xs_moving(a, half))
+                for a in range(PASSES):
+                    nc.tensor.matmul_mx(
+                        base[:], start=(a == 0), stop=(a == PASSES - 1), **stationary(w3_q[a], t), **xs_moving(a, half),
+                    )
                 sums.append(base)
             return sums
 
@@ -270,39 +249,42 @@ def tile_list_suit_loop_contrast_kernel(
                 )
             return dst
 
-        def score(moving, b, c0, c1, engine):
-            scores = bank(b, [P, 2, c1 - c0], "scores%d" % c0)
-            for j in range(2):
+        out_rows = out.rearrange("(j p) s -> p j s", p=P)
+
+        def score(quarter, moving, copy):
+            scores = bank(quarter, [P, N // P, QUARTER], "scores%d" % quarter)
+            for j in range(N // P):
                 cols = slice(P * j, P * (j + 1))
                 nc.tensor.matmul_mx(
                     scores[:, j, :], lhsT=w4_codes[:, cols].bitcast(FP8X4), lhsT_scale=w4_plane[:, cols],
                     start=True, stop=True, **moving,
                 )
-            result = sbuf([P, 2, c1 - c0], F32, "result%d" % c0)
-            copy_on(engine, result[:], scores[:])
-            nc.sync.dma_start(out_rows[:, :, c0:c1], result[:])
+            result = sbuf([P, N // P, QUARTER], F32, "result%d" % quarter)
+            copy(result[:], scores[:])
+            nc.sync.dma_start(out_rows[:, :, QUARTER * quarter : QUARTER * (quarter + 1)], result[:])
 
-        h_bf0 = hidden(0, None, (1,))
-        w2_q = quantise_weight("w2", [("vector", w2_raw, 0, 0, PACK)], 1)
-        h_moving0 = weave_and_quantise(("vector",), h_bf0[:], "h0")
-        h_bf1 = hidden(1, None)
+        h_bf0 = hidden(0, (1,))
+        w2_q = quantise_weight("w2", w2_raw, (on_vector,), 1)
+        h_moving0 = weave_and_quantise(on_vector, h_bf0[:], "h0")
+        h_bf1 = hidden(1, ())
         w3_q = [
-            quantise_weight("w3_0", [("vector", w3_raw0, 0, 0, PACK)], 1),
-            quantise_weight("w3_1", [("vector", w3_raw1, 0, 0, PACK)], 2),
+            quantise_weight("w3_0", w3_raw[0], (on_vector,), 1),
+            quantise_weight("w3_1", w3_raw[1], (on_vector,), 2),
         ]
-        h_moving1 = weave_and_quantise(("scalar",), h_bf1[:], "h1")
+        h_moving1 = weave_and_quantise(on_scalar, h_bf1[:], "h1")
         joint(0, h_moving0)
-        sums0 = base_sums(0)
+        base0 = base_sums(0)
         joint(1, h_moving1)
-        diff0 = contrast(0, sums0, 0, HALF)
-        sums1 = base_sums(1)
-        moving0 = weave_and_quantise(("vector",), diff0[:, :, 0:QUARTER], "diff0")
-        diff2 = contrast(1, sums1, 0, QUARTER)
-        score(moving0, 0, 0, QUARTER, "scalar")
-        moving1 = weave_and_quantise(("scalar",), diff0[:, :, QUARTER:HALF], "diff1")
-        diff3 = contrast(1, sums1, QUARTER, HALF)
-        score(moving1, 1, QUARTER, HALF, "scalar")
-        moving2 = weave_and_quantise(("scalar",), diff2[:], "diff2")
-        moving3 = weave_and_quantise(("vector",), diff3[:], "diff3")
-        score(moving2, 2, HALF, HALF + QUARTER, "scalar")
-        score(moving3, 3, HALF + QUARTER, S, "vector")
+
+        diff_first_half = contrast(0, base0, 0, HALF)
+        base1 = base_sums(1)
+        moving0 = weave_and_quantise(on_vector, diff_first_half[:, :, 0:QUARTER], "diff0")
+        diff2 = contrast(1, base1, 0, QUARTER)
+        score(0, moving0, on_scalar)
+        moving1 = weave_and_quantise(on_scalar, diff_first_half[:, :, QUARTER:HALF], "diff1")
+        diff3 = contrast(1, base1, QUARTER, HALF)
+        score(1, moving1, on_scalar)
+        moving2 = weave_and_quantise(on_scalar, diff2[:], "diff2")
+        moving3 = weave_and_quantise(on_vector, diff3[:], "diff3")
+        score(2, moving2, on_scalar)
+        score(3, moving3, on_vector)

from contextlib import ExitStack

import concourse.mybir as mybir

K, T, S, H, M, N = 1024, 4096, 1024, 512, 512, 256
FLOPS = 2 * S * (2 * K * H + H * M + K * M + M * N)

F32 = mybir.dt.float32
BF16 = mybir.dt.bfloat16
I32 = mybir.dt.int32
U32 = mybir.dt.uint32
U16 = mybir.dt.uint16
U8 = mybir.dt.uint8
FP8X4 = mybir.dt.float8_e4m3fn_x4
FP4X4 = mybir.dt.float4_e2m1fn_x4
ACT = mybir.ActivationFunctionType
ALU = mybir.AluOpType

P = 128
PACK = 4
KP = P * PACK
QUADRANT = 32
PLANE_ROWS = 4
BLOCKS = 16
PASSES = K // KP
HALF = S // 2
QUARTER = S // 4
RUN = 4
ROW_STEP = 4
PICKED_START = (4, 8)


def tile_list_suit_loop_contrast_kernel(
    tc, tab_words, tab_scales, offs, xs_words, xs_scales, w1, wx_words, wx_scales,
    b1, w2, b2, gain, w3, w4_words, w4_scales, out,
):
    nc = tc.nc
    with ExitStack() as ctx:
        keep = ctx.enter_context(tc.tile_pool(name="keep", bufs=1))
        psum = ctx.enter_context(tc.psum_pool(name="psum", bufs=1))

        reuses = {"h0_woven": "w2_raw", "h1_codes": "w3_raw1"}

        def sbuf(shape, dtype, name):
            return keep.tile(shape, dtype, name=name, tag=reuses.get(name, name), align_bytes=64)

        def bank(b, shape, name):
            return psum.tile(shape, F32, name=name, tag="bank%d" % b)

        offsets = keep.tile([P, S // 16], U16, name="offsets")
        nc.sync.dma_start(offsets[:], offs)

        wx_plane_raw = sbuf([P, PASSES, H], U8, "wx_plane_raw")
        xs_plane = sbuf([P, PASSES, S], U8, "xs_plane")
        tab_rows = sbuf([P, T], U8, "tab_rows")
        picked_plane = [sbuf([P, S], U8, "picked_plane%d" % a) for a in range(PASSES)]
        w4_plane = sbuf([P, N], U8, "w4_plane")
        nc.vector.memset(tab_rows[:].bitcast(I32), 0)
        for a in range(PASSES):
            nc.vector.memset(picked_plane[a][:].bitcast(I32), 0)
        nc.gpsimd.memset(wx_plane_raw[:].bitcast(I32), 0)
        nc.gpsimd.memset(xs_plane[:].bitcast(I32), 0)
        nc.vector.memset(w4_plane[:].bitcast(I32), 0)

        def load_xs(half):
            codes = sbuf([P, PASSES, HALF], I32, "xs_codes%d" % half)
            words = xs_words.rearrange("a p c i -> p a (c i)").bitcast(I32)
            nc.sync.dma_start(codes[:], words[:, :, HALF * half : HALF * (half + 1)])
            return codes

        def load_table(a):
            words = sbuf([P, T], I32, "tab_codes%d" % a)
            nc.sync.dma_start(words[:], tab_words[a].rearrange("p t i -> p (t i)").bitcast(I32))
            return words

        def load_weight(w, a, name):
            raw = sbuf([P, PACK, KP], F32, name)
            nc.sync.dma_start(raw[:], w[KP * a : KP * (a + 1), :].rearrange("(p i) c -> p i c", i=PACK))
            return raw

        def load_channel_vector(vec, name):
            dst = sbuf([P, PACK], F32, name)
            nc.sync.dma_start(dst[:], vec.rearrange("(p t) -> p t", t=PACK))
            return dst

        def load_plane_rows(plane, scales):
            for r in range(PLANE_ROWS):
                nc.sync.dma_start(
                    plane[r:P:QUADRANT, :, :].bitcast(I32),
                    scales[:, r:BLOCKS:PLANE_ROWS, :].rearrange("a q c -> q a c").bitcast(I32),
                )

        def place_picked_rows(a):
            step = ROW_STEP * PLANE_ROWS
            for r in range(PLANE_ROWS):
                first = ROW_STEP * (BLOCKS * a + r)
                nc.sync.dma_start(
                    picked_plane[a][PICKED_START[a] + r : P : QUADRANT, :].bitcast(I32),
                    picked_rows[first : first + 3 * step + 1 : step, :].bitcast(I32),
                )

        nc.sync.dma_start(tab_rows[0:P:ROW_STEP, :].bitcast(I32), tab_scales.rearrange("a q c -> (a q) c").bitcast(I32))
        picked_rows = sbuf([P, S], U8, "picked_rows")
        nc.vector.tensor_copy(picked_rows[:], tab_rows[:].indirect(offsets[:]))
        xs_codes = [load_xs(0)]
        wx_raw = sbuf([P, PASSES, 2 * H], U8, "wx_raw")
        nc.sync.dma_start(wx_raw[:].bitcast(I32), wx_words.rearrange("a p c -> p a c").bitcast(I32))
        w1_raw = [load_weight(w1, 0, "w1_raw0")]
        load_plane_rows(wx_plane_raw, wx_scales)
        tab = [load_table(0)]
        place_picked_rows(0)
        tab.append(load_table(1))
        load_plane_rows(xs_plane, xs_scales)
        w1_raw.append(load_weight(w1, 1, "w1_raw1"))
        place_picked_rows(1)
        w2_raw = load_weight(w2, 0, "w2_raw")
        b1_sb = load_channel_vector(b1, "b1_sb")
        xs_codes.append(load_xs(1))
        b2_sb = load_channel_vector(b2, "b2_sb")
        gain_sb = load_channel_vector(gain, "gain_sb")
        w3_raw = [load_weight(w3, a, "w3_raw%d" % a) for a in range(PASSES)]
        w4_codes = sbuf([P, N], I32, "w4_codes")
        nc.sync.dma_start(w4_codes[:], w4_words[0].rearrange("p c i -> p (c i)").bitcast(I32))
        for r in range(PLANE_ROWS):
            nc.sync.dma_start(w4_plane[r:P:QUADRANT, :].bitcast(I32), w4_scales[0, r:BLOCKS:PLANE_ROWS, :].bitcast(I32))

        on_vector = nc.vector.tensor_copy
        on_scalar = nc.scalar.copy

        def quantise_weight(name, raw, copies, calls):
            grouped = sbuf([P, PACK, P, PACK], BF16, name + "_bf")
            codes = sbuf([P, KP], I32, name + "_codes")
            plane = sbuf([P, KP], U8, name + "_plane")
            src = raw[:].rearrange("p i (c t) -> p c i t", t=PACK)
            share = PACK // len(copies)
            for s, copy in enumerate(copies):
                tiles = slice(share * s, share * (s + 1))
                copy(grouped[:, tiles, :, :].rearrange("p t c i -> p c i t"), src[:, :, :, tiles])
            flat = grouped[:].rearrange("p t c i -> p (t c i)")
            width = KP // calls
            for first in range(0, KP, width):
                nc.vector.quantize_mx(
                    codes[:, first : first + width].bitcast(FP8X4), plane[:, first : first + width],
                    flat[:, PACK * first : PACK * (first + width)],
                )
            return codes, plane

        def stationary(quantised, t):
            codes, plane = quantised
            cols = slice(P * t, P * (t + 1))
            return dict(lhsT=codes[:, cols].bitcast(FP8X4), lhsT_scale=plane[:, cols])

        def xs_moving(a, half):
            cols = slice(HALF * half, HALF * (half + 1))
            return dict(rhs=xs_codes[half][:, a, :].bitcast(FP8X4), rhs_scale=xs_plane[:, a, cols])

        wx_codes = sbuf([P, PASSES, 2 * H], U8, "wx_codes")
        wx_plane = sbuf([P, PASSES, H], U8, "wx_plane")
        nc.vector.tensor_copy(
            wx_codes[:].rearrange("p a (t c b) -> p a t c b", t=PACK, b=2),
            wx_raw[:].rearrange("p a (c t b) -> p a t c b", t=PACK, b=2),
        )
        nc.vector.tensor_copy(
            wx_plane[:].rearrange("p a (t c) -> p a t c", t=PACK),
            wx_plane_raw[:].rearrange("p a (c t) -> p a t c", t=PACK),
        )

        h_sum = [[bank(PACK * half + t, [P, HALF], "h_sum%d_%d" % (half, t)) for t in range(PACK)] for half in range(2)]

        def telemetry_passes(half, t, closes):
            for a in range(PASSES):
                nc.tensor.matmul_mx(
                    h_sum[half][t][:],
                    lhsT=wx_codes[:, a, 2 * P * t : 2 * P * (t + 1)].bitcast(FP4X4),
                    lhsT_scale=wx_plane[:, a, P * t : P * (t + 1)],
                    start=False, stop=(closes and a == PASSES - 1), **xs_moving(a, half),
                )

        def table_pass(a, half, t, closes):
            cols = slice(HALF * half, HALF * (half + 1))
            nc.tensor.matmul_mx(
                h_sum[half][t][:],
                rhs=picked[a][:, cols].bitcast(FP8X4),
                rhs_scale=picked_plane[a][PICKED_START[a] : P, cols],
                start=(a == 0), stop=closes, **stationary(w1_q[a], t),
            )

        picked = [sbuf([P, S], I32, "picked%d" % a) for a in range(PASSES)]
        nc.vector.tensor_copy(picked[0][:].bitcast(U32), tab[0][:].bitcast(U32).indirect(offsets[:]))
        w1_q = [quantise_weight("w1_0", w1_raw[0], (on_scalar,), 1)]
        for half in range(2):
            for t in range(PACK):
                table_pass(0, half, t, False)
        for t in range(PACK):
            telemetry_passes(0, t, False)
        nc.vector.tensor_copy(picked[1][:].bitcast(U32), tab[1][:].bitcast(U32).indirect(offsets[:]))
        w1_q.append(quantise_weight("w1_1", w1_raw[1], (on_vector, on_scalar), 2))
        for t in range(PACK):
            table_pass(1, 0, t, True)
        for t in range(PACK):
            table_pass(1, 1, t, False)
            telemetry_passes(1, t, True)

        def weave_and_quantise(copy, tiles, name):
            width = tiles.shape[2]
            woven = sbuf([P, width, PACK], BF16, name + "_woven")
            copy(
                woven[:].rearrange("p (c i) t -> p c t i", i=RUN),
                tiles.rearrange("p t (c i) -> p c t i", i=RUN),
            )
            codes = sbuf([P, width], I32, name + "_codes")
            plane = sbuf([P, width], U8, name + "_plane")
            nc.vector.quantize_mx(codes[:].bitcast(FP8X4), plane[:], woven[:].rearrange("p c t -> p (c t)"))
            return dict(rhs=codes[:].bitcast(FP8X4), rhs_scale=plane[:])

        def hidden(half, vector_tiles):
            h_bf = sbuf([P, PACK, HALF], BF16, "h_bf%d" % half)
            for t in range(PACK):
                if t in vector_tiles:
                    nc.vector.tensor_scalar(h_bf[:, t, :], h_sum[half][t][:], b1_sb[:, t : t + 1], 0.0, ALU.add, ALU.max)
                else:
                    nc.scalar.activation(h_bf[:, t, :], h_sum[half][t][:], ACT.Relu, bias=b1_sb[:, t : t + 1])
            return h_bf

        bounded = [sbuf([P, PACK, HALF], F32, "bounded%d" % half) for half in range(2)]

        def joint(half, moving):
            for t in range(PACK):
                e_sum = bank(t, [P, HALF], "e_sum%d_%d" % (half, t))
                nc.tensor.matmul_mx(e_sum[:], start=True, stop=True, **stationary(w2_q, t), **moving)
                nc.scalar.activation(bounded[half][:, t, :], e_sum[:], ACT.Tanh, bias=b2_sb[:, t : t + 1])

        def base_sums(half):
            sums = []
            for t in range(PACK):
                base = bank(PACK + t, [P, HALF], "base%d_%d" % (half, t))
                for a in range(PASSES):
                    nc.tensor.matmul_mx(
                        base[:], start=(a == 0), stop=(a == PASSES - 1), **stationary(w3_q[a], t), **xs_moving(a, half),
                    )
                sums.append(base)
            return sums

        def contrast(half, sums, c0, c1):
            dst = sbuf([P, PACK, c1 - c0], BF16, "diff_bf%d_%d" % (half, c0))
            for t in range(PACK):
                nc.vector.scalar_tensor_tensor(
                    dst[:, t, :], bounded[half][:, t, c0:c1], gain_sb[:, t : t + 1], sums[t][:, c0:c1], ALU.mult, ALU.subtract,
                )
            return dst

        out_rows = out.rearrange("(j p) s -> p j s", p=P)

        def score(quarter, moving, copy):
            scores = bank(quarter, [P, N // P, QUARTER], "scores%d" % quarter)
            for j in range(N // P):
                cols = slice(P * j, P * (j + 1))
                nc.tensor.matmul_mx(
                    scores[:, j, :], lhsT=w4_codes[:, cols].bitcast(FP8X4), lhsT_scale=w4_plane[:, cols],
                    start=True, stop=True, **moving,
                )
            result = sbuf([P, N // P, QUARTER], F32, "result%d" % quarter)
            copy(result[:], scores[:])
            nc.sync.dma_start(out_rows[:, :, QUARTER * quarter : QUARTER * (quarter + 1)], result[:])

        h_bf0 = hidden(0, (1,))
        w2_q = quantise_weight("w2", w2_raw, (on_vector,), 1)
        h_moving0 = weave_and_quantise(on_vector, h_bf0[:], "h0")
        h_bf1 = hidden(1, ())
        w3_q = [
            quantise_weight("w3_0", w3_raw[0], (on_vector,), 1),
            quantise_weight("w3_1", w3_raw[1], (on_vector,), 2),
        ]
        h_moving1 = weave_and_quantise(on_scalar, h_bf1[:], "h1")
        joint(0, h_moving0)
        base0 = base_sums(0)
        joint(1, h_moving1)

        diff_first_half = contrast(0, base0, 0, HALF)
        base1 = base_sums(1)
        moving0 = weave_and_quantise(on_vector, diff_first_half[:, :, 0:QUARTER], "diff0")
        diff2 = contrast(1, base1, 0, QUARTER)
        score(0, moving0, on_scalar)
        moving1 = weave_and_quantise(on_scalar, diff_first_half[:, :, QUARTER:HALF], "diff1")
        diff3 = contrast(1, base1, QUARTER, HALF)
        score(1, moving1, on_scalar)
        moving2 = weave_and_quantise(on_scalar, diff2[:], "diff2")
        moving3 = weave_and_quantise(on_vector, diff3[:], "diff3")
        score(2, moving2, on_scalar)
        score(3, moving3, on_vector)
